import numpy as np, ml_dtypes
CORES = [56,64,184,192,312,320,440,448]
N = 8
F, TK = 64, 64
def setup_inputs(rng):
    return {"x": rng.standard_normal((N, 128, N * TK), dtype=np.float32).astype(ml_dtypes.bfloat16), "w": rng.standard_normal((N, 128, F), dtype=np.float32).astype(ml_dtypes.bfloat16)}
def setup_inputs_big(rng):
    d = setup_inputs(rng)
    for k in ("x", "w"): d[k] = (d[k].astype(np.float32) * 1024.0).astype(d[k].dtype)
    return d
def setup_inputs_small(rng):
    d = setup_inputs(rng)
    for k in ("x", "w"): d[k] = (d[k].astype(np.float32) * (1 / 1024.0)).astype(d[k].dtype)
    return d
def setup_inputs_apart(rng):
    d = setup_inputs(rng)
    f = (10.0 ** rng.permutation(np.linspace(-1.5, 1.5, N))).astype(np.float32).reshape(N, 1, 1)
    for k in ("x", "w"): d[k] = (d[k].astype(np.float32) * f).astype(d[k].dtype)
    return d
def reference(x, w):
    X, W = x.astype(np.float64), w.astype(np.float64)
    y = np.zeros((N, F, N * TK))
    for r in range(N):
        for j in range(N):
            y[r][:, TK * j:TK * j + TK] = W[r].T @ X[j][:, TK * r:TK * r + TK]
    return {"y": y.astype(ml_dtypes.bfloat16 if x.dtype != np.float64 else np.float64)}

@@ -1,0 +1,161 @@
+from concourse.bass import DstId, RemoteDMATransfer
+
+BLK = 64
+NENG = 4
+
+SCRATCH = {
+    "xs": ("sbuf", [128, 512], "bfloat16"),
+    "ws": ("sbuf", [128, 64], "bfloat16"),
+    "xr": ("sbuf", [128, 512], "bfloat16"),
+    "hp": ("sbuf", [128, 128], "bfloat16"),
+    "ys": ("sbuf", [128, 512], "bfloat16"),
+    "psA": ("psum", [128, 512], "float32"),
+    "psB": ("psum", [128, 512], "float32"),
+}
+SEMAPHORES = ["ldx", "ldw", "sent", "harr", "hsent", "arrA", "arrB", "mmA", "mmB", "cpA", "cpB", "stA", "stB"]
+
+
+def _bits(m):
+    return [b for b in range(m.bit_length()) if (m >> b) & 1]
+
+
+def _deal(topo, core, dsts, n):
+    allowed = [topo.mask(core, d) for d in dsts]
+    common = allowed[0]
+    for a in allowed:
+        common &= a
+    if n * len(dsts) <= len(_bits(common)):
+        groups = [(common, list(range(len(dsts))))]
+    else:
+        kinds = sorted(set(allowed), key=lambda a: len(_bits(a)))
+        groups = [(a, [i for i in range(len(dsts)) if allowed[i] == a]) for a in kinds]
+    masks, used = [0] * len(dsts), 0
+    for a, idx in groups:
+        free = [b for b in _bits(a) if not (used >> b) & 1][: n * len(idx)]
+        for t, i in enumerate(idx):
+            for b in free[t::len(idx)]:
+                masks[i] |= 1 << b
+                used |= 1 << b
+    return masks
+
+
+def _send(g, topo, core, items, n, local_sem):
+    masks = _deal(topo, core, [it[0] for it in items], n)
+    trs = []
+    for (d, src, dst, sem), m in zip(items, masks):
+        rid, pid = topo.addr(d, core)
+        trs.append(RemoteDMATransfer(dst_ids=[DstId(rid=rid, pnc=pid)], dma_engine_mask=m, remote_sem=sem, src=src, dst=dst))
+    g.remote_dma_fused(trs, local_sem=local_sem)
+    return n * len(items)
+
+
+def rank_program(g, core, T, topo):
+    cores = list(T.cores)
+    home = [c for c in cores if topo.host(c) == topo.host(core) and topo.chip(c) == topo.chip(core)]
+    if not home:
+        return
+    R = home[0]
+    n_world = topo.CORES_PER_HOST * (max(topo.host(c) for c in cores) + 1)
+
+    def at(h, like):
+        return [c for c in cores if topo.host(c) == h and topo.chip(c) == topo.chip(like)][0]
+
+    def twin(c):
+        return [d for d in cores if topo.host(d) == topo.host(c) and d != c][0]
+
+    def hosts_of(c):
+        h = topo.host(c)
+        others = sorted({topo.host(d) for d in cores} - {h})
+        peer = [k for k in others if topo.rack(k) == topo.rack(h)][0]
+        cab = [k for k in others if topo.rack(k) != topo.rack(h) and topo.may_write(c, at(k, c))][0]
+        diag = [k for k in others if not topo.may_write(c, at(k, c))][0]
+        return peer, cab, diag
+
+    def roles(c):
+        own = [k for k in range(n_world) if k != c and topo.host(k) == topo.host(c) and topo.chip(k) == topo.chip(c)
+               and topo.may_write(k, twin(c))]
+        near = [k for k in own if topo.die(k) == topo.die(c)]
+        far = [k for k in own if topo.die(k) != topo.die(c)]
+        return {"cab": near[0], "diag": near[1], "peer": far[0], "twin": far[1]}
+
+    def pair(h):
+        return sorted(T.rank_of(c) for c in cores if topo.host(c) == h)
+
+    def same_rack(a, b):
+        return topo.rack(topo.host(a)) == topo.rack(topo.host(b))
+
+    sem = T.sem
+    peer, cab, diag = hosts_of(R)
+
+    if core != R:
+        role = [name for name, k in roles(R).items() if k == core]
+        if not role:
+            return
+        role = role[0]
+        if role == "cab":
+            src, dsth = at(cab, R), topo.host(R)
+        elif role == "diag":
+            src = at(peer, R)
+            dsth = hosts_of(src)[2]
+        elif role == "peer":
+            src, dsth = R, peer
+        else:
+            src, dsth = R, topo.host(R)
+        s = T.rank_of(src)
+        items = []
+        for t, j in enumerate(pair(dsth)):
+            d = cores[j]
+            if d == src:
+                continue
+            items.append((d, T.hp[:, BLK * t:BLK * (t + 1)], T.xr[:, BLK * s:BLK * (s + 1)],
+                          sem.arrA if same_rack(d, src) else sem.arrB))
+        g.wait_ge(sem.harr, NENG)
+        left = _send(g, topo, core, items, NENG, sem.hsent)
+        g.wait_ge(sem.hsent, left)
+        return
+
+    i = T.rank_of(core)
+    g.sync.dma_start(T.xs[:, :], T.x[:, :]).then_inc(sem.ldx, 16)
+    g.sync.dma_start(T.ws[:, :], T.w[:, :]).then_inc(sem.ldw, 16)
+
+    mine = roles(R)
+    plan = [(roles(at(cab, R))["cab"], cab), (roles(at(peer, R))["diag"], diag),
+            (mine["peer"], peer), (mine["twin"], topo.host(R))]
+    items = []
+    for k, h in plan:
+        rs = pair(h)
+        items.append((k, T.xs[:, BLK * rs[0]:BLK * (rs[-1] + 1)], T.hp[:, :], sem.harr))
+    g.wait_ge(sem.ldx, 16)
+    left = _send(g, topo, core, items, NENG, sem.sent)
+
+    A = sorted(j for j in range(len(cores)) if same_rack(cores[j], R))
+    B = sorted(j for j in range(len(cores)) if not same_rack(cores[j], R))
+    a0, b0 = A[0], B[0]
+    w = T.ws[:, :]
+
+    te, ve = g.tensor, g.vector
+    te.wait_ge(sem.ldx, 16)
+    te.wait_ge(sem.ldw, 16)
+    te.matmul(T.psA[0:64, BLK * (i - a0):BLK * (i - a0 + 1)], w, T.xs[:, BLK * i:BLK * (i + 1)], True, True).then_inc(sem.mmA, 1)
+    nA = 1
+    te.wait_ge(sem.arrA, NENG * (len(A) - 1))
+    for lo, hi in ((a0, i), (i + 1, A[-1] + 1)):
+        if hi > lo:
+            te.matmul(T.psA[0:64, BLK * (lo - a0):BLK * (hi - a0)], w, T.xr[:, BLK * lo:BLK * hi], True, True).then_inc(sem.mmA, 1)
+            nA += 1
+    te.wait_ge(sem.arrB, NENG * len(B))
+    te.matmul(T.psB[0:64, 0:BLK * len(B)], w, T.xr[:, BLK * b0:BLK * (B[-1] + 1)], True, True).then_inc(sem.mmB, 1)
+
+    ca, cb = (BLK * a0, BLK * (A[-1] + 1)), (BLK * b0, BLK * (B[-1] + 1))
+    ve.wait_ge(sem.mmA, nA)
+    ve.tensor_copy(T.ys[0:64, ca[0]:ca[1]], T.psA[0:64, 0:BLK * len(A)]).then_inc(sem.cpA, 1)
+    ve.wait_ge(sem.mmB, 1)
+    ve.tensor_copy(T.ys[0:64, cb[0]:cb[1]], T.psB[0:64, 0:BLK * len(B)]).then_inc(sem.cpB, 1)
+
+    g.sync.wait_ge(sem.cpA, 1)
+    g.sync.dma_start(T.y[:, ca[0]:ca[1]], T.ys[0:64, ca[0]:ca[1]]).then_inc(sem.stA, 16)
+    g.scalar.wait_ge(sem.cpB, 1)
+    g.scalar.dma_start(T.y[:, cb[0]:cb[1]], T.ys[0:64, cb[0]:cb[1]]).then_inc(sem.stB, 16)
+    g.sync.wait_ge(sem.stA, 16)
+    g.scalar.wait_ge(sem.stB, 16)
+    g.wait_ge(sem.sent, left)

@@ -1,52 +1,42 @@
 from concourse.bass import DstId, RemoteDMATransfer
 
 BLK = 64
-NENG = 4
 
 SCRATCH = {
     "xs": ("sbuf", [128, 512], "bfloat16"),
     "ws": ("sbuf", [128, 64], "bfloat16"),
     "xr": ("sbuf", [128, 512], "bfloat16"),
-    "hp": ("sbuf", [128, 128], "bfloat16"),
+    "dd": ("dram", [5, 128, 64], "bfloat16"),
+    "hd": ("dram", [128, 64], "bfloat16"),
     "ys": ("sbuf", [128, 512], "bfloat16"),
-    "psA": ("psum", [128, 512], "float32"),
-    "psB": ("psum", [128, 512], "float32"),
+    "ps0": ("psum", [128, 512], "float32"),
+    "ps1": ("psum", [128, 512], "float32"),
+    "ps2": ("psum", [128, 512], "float32"),
+    "ps3": ("psum", [128, 512], "float32"),
 }
-SEMAPHORES = ["ldx", "ldw", "sent", "harr", "hsent", "arrA", "arrB", "mmA", "mmB", "cpA", "cpB", "stA", "stB"]
+SEMAPHORES = ["ld1", "ldx", "ldw", "sent", "harr", "hsent", "arrS", "arrD", "arrG",
+              "mm0", "mm1", "mm2", "mm3", "cp", "st"]
 
 
 def _bits(m):
     return [b for b in range(m.bit_length()) if (m >> b) & 1]
 
 
-def _deal(topo, core, dsts, n):
-    allowed = [topo.mask(core, d) for d in dsts]
-    common = allowed[0]
-    for a in allowed:
-        common &= a
-    if n * len(dsts) <= len(_bits(common)):
-        groups = [(common, list(range(len(dsts))))]
-    else:
-        kinds = sorted(set(allowed), key=lambda a: len(_bits(a)))
-        groups = [(a, [i for i in range(len(dsts)) if allowed[i] == a]) for a in kinds]
-    masks, used = [0] * len(dsts), 0
-    for a, idx in groups:
-        free = [b for b in _bits(a) if not (used >> b) & 1][: n * len(idx)]
-        for t, i in enumerate(idx):
-            for b in free[t::len(idx)]:
-                masks[i] |= 1 << b
-                used |= 1 << b
-    return masks
+def _mask(engines):
+    m = 0
+    for b in engines:
+        m |= 1 << b
+    return m
 
 
-def _send(g, topo, core, items, n, local_sem):
-    masks = _deal(topo, core, [it[0] for it in items], n)
+def _send(g, topo, core, items, local_sem):
     trs = []
-    for (d, src, dst, sem), m in zip(items, masks):
+    for d, src, dst, sem, engines in items:
         rid, pid = topo.addr(d, core)
-        trs.append(RemoteDMATransfer(dst_ids=[DstId(rid=rid, pnc=pid)], dma_engine_mask=m, remote_sem=sem, src=src, dst=dst))
+        trs.append(RemoteDMATransfer(dst_ids=[DstId(rid=rid, pnc=pid)], dma_engine_mask=_mask(engines), remote_sem=sem,
+                                     src=src, dst=dst))
     g.remote_dma_fused(trs, local_sem=local_sem)
-    return n * len(items)
+    return sum(len(it[4]) for it in items)
 
 
 def rank_program(g, core, T, topo):
@@ -72,90 +62,96 @@ def rank_program(g, core, T, topo):
         return peer, cab, diag
 
     def roles(c):
-        own = [k for k in range(n_world) if k != c and topo.host(k) == topo.host(c) and topo.chip(k) == topo.chip(c)
-               and topo.may_write(k, twin(c))]
+        chipmates = [k for k in range(n_world) if k != c and topo.host(k) == topo.host(c) and topo.chip(k) == topo.chip(c)]
+        own = [k for k in chipmates if topo.may_write(k, twin(c))]
+        plain = [k for k in chipmates if k not in own and topo.die(k) == topo.die(c)]
         near = [k for k in own if topo.die(k) == topo.die(c)]
         far = [k for k in own if topo.die(k) != topo.die(c)]
-        return {"cab": near[0], "diag": near[1], "peer": far[0], "twin": far[1]}
+        return {"dodd": near[0], "cabo": near[1], "twin": far[0], "peero": far[1], "dsame": plain[0]}
 
-    def pair(h):
-        return sorted(T.rank_of(c) for c in cores if topo.host(c) == h)
+    def plan(c):
+        peer, cab, diag = hosts_of(c)
+        mine = roles(c)
+        return [(at(diag, c), roles(at(peer, c))["dsame"], True),
+                (twin(at(diag, c)), roles(at(cab, c))["dodd"], True),
+                (twin(at(cab, c)), mine["cabo"], False),
+                (twin(at(peer, c)), mine["peero"], False),
+                (twin(c), mine["twin"], False)]
 
-    def same_rack(a, b):
-        return topo.rack(topo.host(a)) == topo.rack(topo.host(b))
+    def feed_engines(c):
+        p = plan(c)
+        allowed = [_bits(topo.mask(c, k)) for d, k, f in p]
+        widest = max(allowed, key=len)
+        order = widest[0::2] + widest[1::2]
+        turn = sorted(range(len(p)), key=lambda t: (len(allowed[t]), topo.die(p[t][1]) == topo.die(c)))
+        eng, used = {}, []
+        for t in turn:
+            eng[t] = [b for b in order if b in allowed[t] and b not in used][:2]
+            used += eng[t]
+        return eng
 
     sem = T.sem
-    peer, cab, diag = hosts_of(R)
 
     if core != R:
-        role = [name for name, k in roles(R).items() if k == core]
-        if not role:
+        jobs = [(c, t) for c in cores for t, (d, k, f) in enumerate(plan(c)) if k == core]
+        if not jobs:
             return
-        role = role[0]
-        if role == "cab":
-            src, dsth = at(cab, R), topo.host(R)
-        elif role == "diag":
-            src = at(peer, R)
-            dsth = hosts_of(src)[2]
-        elif role == "peer":
-            src, dsth = R, peer
-        else:
-            src, dsth = R, topo.host(R)
+        src, t = jobs[0]
+        d, _, first = plan(src)[t]
         s = T.rank_of(src)
-        items = []
-        for t, j in enumerate(pair(dsth)):
-            d = cores[j]
-            if d == src:
-                continue
-            items.append((d, T.hp[:, BLK * t:BLK * (t + 1)], T.xr[:, BLK * s:BLK * (s + 1)],
-                          sem.arrA if same_rack(d, src) else sem.arrB))
-        g.wait_ge(sem.harr, NENG)
-        left = _send(g, topo, core, items, NENG, sem.hsent)
+        g.wait_ge(sem.harr, len(feed_engines(src)[t]))
+        left = _send(g, topo, core, [(d, T.hd[:, :], T.xr[:, BLK * s:BLK * (s + 1)], sem.arrD if first else sem.arrG,
+                                      _bits(topo.mask(core, d)))], sem.hsent)
         g.wait_ge(sem.hsent, left)
         return
 
     i = T.rank_of(core)
-    g.sync.dma_start(T.xs[:, :], T.x[:, :]).then_inc(sem.ldx, 16)
-    g.sync.dma_start(T.ws[:, :], T.w[:, :]).then_inc(sem.ldw, 16)
+    p = plan(R)
+    eng = feed_engines(R)
+    peer, cab, diag = hosts_of(R)
 
-    mine = roles(R)
-    plan = [(roles(at(cab, R))["cab"], cab), (roles(at(peer, R))["diag"], diag),
-            (mine["peer"], peer), (mine["twin"], topo.host(R))]
-    items = []
-    for k, h in plan:
-        rs = pair(h)
-        items.append((k, T.xs[:, BLK * rs[0]:BLK * (rs[-1] + 1)], T.hp[:, :], sem.harr))
+    def blk(buf, j):
+        return buf[:, BLK * j:BLK * (j + 1)]
+
+    queues = [g.sync, g.scalar]
+    for t, (d, k, first) in enumerate(p):
+        queues[t % 2].dma_start(T.dd[t], blk(T.x, T.rank_of(d))).then_inc(sem.ld1, 16)
+    queues[len(p) % 2].dma_start(T.xs[:, :], T.x[:, :]).then_inc(sem.ldx, 16)
+    queues[(len(p) + 1) % 2].dma_start(T.ws[:, :], T.w[:, :]).then_inc(sem.ldw, 16)
+
+    g.wait_ge(sem.ld1, 16 * len(p))
+    left = _send(g, topo, core, [(k, T.dd[t], T.hd[:, :], sem.harr, eng[t]) for t, (d, k, f) in enumerate(p)], sem.sent)
+    direct = [at(peer, R), at(cab, R)]
+    out = _bits(topo.mask(core, direct[0]) & topo.mask(core, direct[1]))
     g.wait_ge(sem.ldx, 16)
-    left = _send(g, topo, core, items, NENG, sem.sent)
+    left += _send(g, topo, core, [(d, blk(T.xs, T.rank_of(d)), blk(T.xr, i), sem.arrS, out[n::len(direct)])
+                                  for n, d in enumerate(direct)], sem.sent)
 
-    A = sorted(j for j in range(len(cores)) if same_rack(cores[j], R))
-    B = sorted(j for j in range(len(cores)) if not same_rack(cores[j], R))
-    a0, b0 = A[0], B[0]
-    w = T.ws[:, :]
+    srcS = sorted(T.rank_of(c) for c in direct)
+    srcD = sorted(T.rank_of(c) for c in cores for d, k, f in plan(c) if d == R and f)
+    srcG = sorted(T.rank_of(c) for c in cores for d, k, f in plan(c) if d == R and not f)
+    n_off = len(out)
+    groups = [(None, 0, [i], T.xs, T.ps0, sem.mm0),
+              (sem.arrS, (n_off // len(direct)) * len(srcS), srcS, T.xr, T.ps1, sem.mm1),
+              (sem.arrD, n_off * len(srcD), srcD, T.xr, T.ps2, sem.mm2),
+              (sem.arrG, n_off * len(srcG), srcG, T.xr, T.ps3, sem.mm3)]
 
     te, ve = g.tensor, g.vector
     te.wait_ge(sem.ldx, 16)
     te.wait_ge(sem.ldw, 16)
-    te.matmul(T.psA[0:64, BLK * (i - a0):BLK * (i - a0 + 1)], w, T.xs[:, BLK * i:BLK * (i + 1)], True, True).then_inc(sem.mmA, 1)
-    nA = 1
-    te.wait_ge(sem.arrA, NENG * (len(A) - 1))
-    for lo, hi in ((a0, i), (i + 1, A[-1] + 1)):
-        if hi > lo:
-            te.matmul(T.psA[0:64, BLK * (lo - a0):BLK * (hi - a0)], w, T.xr[:, BLK * lo:BLK * hi], True, True).then_inc(sem.mmA, 1)
-            nA += 1
-    te.wait_ge(sem.arrB, NENG * len(B))
-    te.matmul(T.psB[0:64, 0:BLK * len(B)], w, T.xr[:, BLK * b0:BLK * (B[-1] + 1)], True, True).then_inc(sem.mmB, 1)
+    for arr, cnt, js, buf, ps, mm in groups:
+        if arr is not None:
+            te.wait_ge(arr, cnt)
+        for n, j in enumerate(js):
+            te.matmul(ps[0:64, BLK * n:BLK * (n + 1)], T.ws[:, :], blk(buf, j), True, True).then_inc(mm, 1)
+    done = 0
+    for arr, cnt, js, buf, ps, mm in groups:
+        ve.wait_ge(mm, len(js))
+        for n, j in enumerate(js):
+            ve.tensor_copy(T.ys[0:64, BLK * j:BLK * (j + 1)], ps[0:64, BLK * n:BLK * (n + 1)]).then_inc(sem.cp, 1)
+            done += 1
 
-    ca, cb = (BLK * a0, BLK * (A[-1] + 1)), (BLK * b0, BLK * (B[-1] + 1))
-    ve.wait_ge(sem.mmA, nA)
-    ve.tensor_copy(T.ys[0:64, ca[0]:ca[1]], T.psA[0:64, 0:BLK * len(A)]).then_inc(sem.cpA, 1)
-    ve.wait_ge(sem.mmB, 1)
-    ve.tensor_copy(T.ys[0:64, cb[0]:cb[1]], T.psB[0:64, 0:BLK * len(B)]).then_inc(sem.cpB, 1)
-
-    g.sync.wait_ge(sem.cpA, 1)
-    g.sync.dma_start(T.y[:, ca[0]:ca[1]], T.ys[0:64, ca[0]:ca[1]]).then_inc(sem.stA, 16)
-    g.scalar.wait_ge(sem.cpB, 1)
-    g.scalar.dma_start(T.y[:, cb[0]:cb[1]], T.ys[0:64, cb[0]:cb[1]]).then_inc(sem.stB, 16)
-    g.sync.wait_ge(sem.stA, 16)
-    g.scalar.wait_ge(sem.stB, 16)
+    g.sync.wait_ge(sem.cp, done)
+    g.sync.dma_start(T.y[:, :], T.ys[0:64, :]).then_inc(sem.st, 16)
+    g.sync.wait_ge(sem.st, 16)
     g.wait_ge(sem.sent, left)

@@ -14,7 +14,7 @@ SCRATCH = {
     "ps2": ("psum", [128, 512], "float32"),
     "ps3": ("psum", [128, 512], "float32"),
 }
-SEMAPHORES = ["ld1", "ldx", "ldw", "sent", "harr", "hsent", "arrS", "arrD", "arrG",
+SEMAPHORES = ["ld0", "ld1", "ldx", "ldw", "sent", "harr", "hsent", "arrS", "arrD", "arrG",
               "mm0", "mm1", "mm2", "mm3", "cp", "st"]
 
 
@@ -72,8 +72,8 @@ def rank_program(g, core, T, topo):
     def plan(c):
         peer, cab, diag = hosts_of(c)
         mine = roles(c)
-        return [(at(diag, c), roles(at(peer, c))["dsame"], True),
-                (twin(at(diag, c)), roles(at(cab, c))["dodd"], True),
+        return [(twin(at(diag, c)), roles(at(cab, c))["dodd"], True),
+                (at(diag, c), roles(at(peer, c))["dsame"], True),
                 (twin(at(cab, c)), mine["cabo"], False),
                 (twin(at(peer, c)), mine["peero"], False),
                 (twin(c), mine["twin"], False)]
@@ -115,12 +115,15 @@ def rank_program(g, core, T, topo):
 
     queues = [g.sync, g.scalar]
     for t, (d, k, first) in enumerate(p):
-        queues[t % 2].dma_start(T.dd[t], blk(T.x, T.rank_of(d))).then_inc(sem.ld1, 16)
+        queues[t % 2].dma_start(T.dd[t], blk(T.x, T.rank_of(d))).then_inc(sem.ld0 if t == 0 else sem.ld1, 16)
     queues[len(p) % 2].dma_start(T.xs[:, :], T.x[:, :]).then_inc(sem.ldx, 16)
     queues[(len(p) + 1) % 2].dma_start(T.ws[:, :], T.w[:, :]).then_inc(sem.ldw, 16)
 
-    g.wait_ge(sem.ld1, 16 * len(p))
-    left = _send(g, topo, core, [(k, T.dd[t], T.hd[:, :], sem.harr, eng[t]) for t, (d, k, f) in enumerate(p)], sem.sent)
+    feeds = [(k, T.dd[t], T.hd[:, :], sem.harr, eng[t]) for t, (d, k, f) in enumerate(p)]
+    g.wait_ge(sem.ld0, 16)
+    left = _send(g, topo, core, feeds[:1], sem.sent)
+    g.wait_ge(sem.ld1, 16 * (len(p) - 1))
+    left += _send(g, topo, core, feeds[1:], sem.sent)
     direct = [at(peer, R), at(cab, R)]
     out = _bits(topo.mask(core, direct[0]) & topo.mask(core, direct[1]))
     g.wait_ge(sem.ldx, 16)

from concourse.bass import DstId, RemoteDMATransfer

BLK = 64

SCRATCH = {
    "xs": ("sbuf", [128, 512], "bfloat16"),
    "ws": ("sbuf", [128, 64], "bfloat16"),
    "xr": ("sbuf", [128, 512], "bfloat16"),
    "dd": ("dram", [5, 128, 64], "bfloat16"),
    "hd": ("dram", [128, 64], "bfloat16"),
    "ys": ("sbuf", [128, 512], "bfloat16"),
    "ps0": ("psum", [128, 512], "float32"),
    "ps1": ("psum", [128, 512], "float32"),
    "ps2": ("psum", [128, 512], "float32"),
    "ps3": ("psum", [128, 512], "float32"),
}
SEMAPHORES = ["ld0", "ld1", "ldx", "ldw", "sent", "harr", "hsent", "arrS", "arrD", "arrG",
              "mm0", "mm1", "mm2", "mm3", "cp", "st"]


def _bits(m):
    return [b for b in range(m.bit_length()) if (m >> b) & 1]


def _mask(engines):
    m = 0
    for b in engines:
        m |= 1 << b
    return m


def _send(g, topo, core, items, local_sem):
    trs = []
    for d, src, dst, sem, engines in items:
        rid, pid = topo.addr(d, core)
        trs.append(RemoteDMATransfer(dst_ids=[DstId(rid=rid, pnc=pid)], dma_engine_mask=_mask(engines), remote_sem=sem,
                                     src=src, dst=dst))
    g.remote_dma_fused(trs, local_sem=local_sem)
    return sum(len(it[4]) for it in items)


def rank_program(g, core, T, topo):
    cores = list(T.cores)
    home = [c for c in cores if topo.host(c) == topo.host(core) and topo.chip(c) == topo.chip(core)]
    if not home:
        return
    R = home[0]
    n_world = topo.CORES_PER_HOST * (max(topo.host(c) for c in cores) + 1)

    def at(h, like):
        return [c for c in cores if topo.host(c) == h and topo.chip(c) == topo.chip(like)][0]

    def twin(c):
        return [d for d in cores if topo.host(d) == topo.host(c) and d != c][0]

    def hosts_of(c):
        h = topo.host(c)
        others = sorted({topo.host(d) for d in cores} - {h})
        peer = [k for k in others if topo.rack(k) == topo.rack(h)][0]
        cab = [k for k in others if topo.rack(k) != topo.rack(h) and topo.may_write(c, at(k, c))][0]
        diag = [k for k in others if not topo.may_write(c, at(k, c))][0]
        return peer, cab, diag

    def roles(c):
        chipmates = [k for k in range(n_world) if k != c and topo.host(k) == topo.host(c) and topo.chip(k) == topo.chip(c)]
        own = [k for k in chipmates if topo.may_write(k, twin(c))]
        plain = [k for k in chipmates if k not in own and topo.die(k) == topo.die(c)]
        near = [k for k in own if topo.die(k) == topo.die(c)]
        far = [k for k in own if topo.die(k) != topo.die(c)]
        return {"dodd": near[0], "cabo": near[1], "twin": far[0], "peero": far[1], "dsame": plain[0]}

    def plan(c):
        peer, cab, diag = hosts_of(c)
        mine = roles(c)
        return [(twin(at(diag, c)), roles(at(cab, c))["dodd"], True),
                (at(diag, c), roles(at(peer, c))["dsame"], True),
                (twin(at(cab, c)), mine["cabo"], False),
                (twin(at(peer, c)), mine["peero"], False),
                (twin(c), mine["twin"], False)]

    def feed_engines(c):
        p = plan(c)
        allowed = [_bits(topo.mask(c, k)) for d, k, f in p]
        widest = max(allowed, key=len)
        order = widest[0::2] + widest[1::2]
        turn = sorted(range(len(p)), key=lambda t: (len(allowed[t]), topo.die(p[t][1]) == topo.die(c)))
        eng, used = {}, []
        for t in turn:
            eng[t] = [b for b in order if b in allowed[t] and b not in used][:2]
            used += eng[t]
        return eng

    sem = T.sem

    if core != R:
        jobs = [(c, t) for c in cores for t, (d, k, f) in enumerate(plan(c)) if k == core]
        if not jobs:
            return
        src, t = jobs[0]
        d, _, first = plan(src)[t]
        s = T.rank_of(src)
        g.wait_ge(sem.harr, len(feed_engines(src)[t]))
        left = _send(g, topo, core, [(d, T.hd[:, :], T.xr[:, BLK * s:BLK * (s + 1)], sem.arrD if first else sem.arrG,
                                      _bits(topo.mask(core, d)))], sem.hsent)
        g.wait_ge(sem.hsent, left)
        return

    i = T.rank_of(core)
    p = plan(R)
    eng = feed_engines(R)
    peer, cab, diag = hosts_of(R)

    def blk(buf, j):
        return buf[:, BLK * j:BLK * (j + 1)]

    queues = [g.sync, g.scalar]
    for t, (d, k, first) in enumerate(p):
        queues[t % 2].dma_start(T.dd[t], blk(T.x, T.rank_of(d))).then_inc(sem.ld0 if t == 0 else sem.ld1, 16)
    queues[len(p) % 2].dma_start(T.xs[:, :], T.x[:, :]).then_inc(sem.ldx, 16)
    queues[(len(p) + 1) % 2].dma_start(T.ws[:, :], T.w[:, :]).then_inc(sem.ldw, 16)

    feeds = [(k, T.dd[t], T.hd[:, :], sem.harr, eng[t]) for t, (d, k, f) in enumerate(p)]
    g.wait_ge(sem.ld0, 16)
    left = _send(g, topo, core, feeds[:1], sem.sent)
    g.wait_ge(sem.ld1, 16 * (len(p) - 1))
    left += _send(g, topo, core, feeds[1:], sem.sent)
    direct = [at(peer, R), at(cab, R)]
    out = _bits(topo.mask(core, direct[0]) & topo.mask(core, direct[1]))
    g.wait_ge(sem.ldx, 16)
    left += _send(g, topo, core, [(d, blk(T.xs, T.rank_of(d)), blk(T.xr, i), sem.arrS, out[n::len(direct)])
                                  for n, d in enumerate(direct)], sem.sent)

    srcS = sorted(T.rank_of(c) for c in direct)
    srcD = sorted(T.rank_of(c) for c in cores for d, k, f in plan(c) if d == R and f)
    srcG = sorted(T.rank_of(c) for c in cores for d, k, f in plan(c) if d == R and not f)
    n_off = len(out)
    groups = [(None, 0, [i], T.xs, T.ps0, sem.mm0),
              (sem.arrS, (n_off // len(direct)) * len(srcS), srcS, T.xr, T.ps1, sem.mm1),
              (sem.arrD, n_off * len(srcD), srcD, T.xr, T.ps2, sem.mm2),
              (sem.arrG, n_off * len(srcG), srcG, T.xr, T.ps3, sem.mm3)]

    te, ve = g.tensor, g.vector
    te.wait_ge(sem.ldx, 16)
    te.wait_ge(sem.ldw, 16)
    for arr, cnt, js, buf, ps, mm in groups:
        if arr is not None:
            te.wait_ge(arr, cnt)
        for n, j in enumerate(js):
            te.matmul(ps[0:64, BLK * n:BLK * (n + 1)], T.ws[:, :], blk(buf, j), True, True).then_inc(mm, 1)
    done = 0
    for arr, cnt, js, buf, ps, mm in groups:
        ve.wait_ge(mm, len(js))
        for n, j in enumerate(js):
            ve.tensor_copy(T.ys[0:64, BLK * j:BLK * (j + 1)], ps[0:64, BLK * n:BLK * (n + 1)]).then_inc(sem.cp, 1)
            done += 1

    g.sync.wait_ge(sem.cp, done)
    g.sync.dma_start(T.y[:, :], T.ys[0:64, :]).then_inc(sem.st, 16)
    g.sync.wait_ge(sem.st, 16)
    g.wait_ge(sem.sent, left)
